import numpy as np
import ml_dtypes


def mxq(x, axis, fmt="e4m3"):
    dtype, down = {"e4m3": (ml_dtypes.float8_e4m3fn, 7), "e5m2": (ml_dtypes.float8_e5m2, 14)}[fmt]
    v = np.moveaxis(np.asarray(x, np.float32).astype(ml_dtypes.bfloat16).astype(np.float64), axis, -1)
    blocks = v.reshape(v.shape[:-1] + (-1, 32))
    amax = np.abs(blocks).max(-1, keepdims=True)
    byte = np.maximum(np.where(amax > 0, np.frexp(amax)[1] - 1 + 127, 0) - down, 1)
    scale = np.exp2(byte - 127.0)
    codes = (blocks / scale).astype(np.float32).astype(dtype).astype(np.float64)
    return np.moveaxis((codes * scale).reshape(v.shape), -1, axis)


WIDE = False


def mx_kscale(k):
    if not WIDE:
        return np.ones(k)
    levels = np.array([10, -10, 5, -5, 0])
    if k % 512:
        return np.exp2(np.random.permutation(np.resize(levels, k // 32))).repeat(32)
    a = np.empty((k // 512, 16))
    for p in range(k // 512):
        a[p, :8] = np.random.permutation(np.resize(levels, 8))
        for g in range(8):
            far = levels[np.abs(levels - a[p, g]) >= 10]
            a[p, g + 8] = far[np.random.randint(len(far))]
    return np.exp2(a.ravel()).repeat(32)


def f64(x):
    return np.asarray(x).astype(np.float64)


def striped(idx):
    return np.tile(idx.reshape(-1, 16).T, (8, 1)).astype(np.uint16)


def unstriped(offs):
    return offs[:16].T.reshape(-1).astype(np.int64)


def pack_weight(w):
    k, n = w.shape
    w = f64(np.asarray(w, np.float32).astype(ml_dtypes.bfloat16)).reshape(k // 32, 32, n)
    amax = np.abs(w).max(1)
    byte = np.clip(np.where(amax > 0, np.frexp(amax)[1] - 1 + 127 - 7, 1), 1, 254)
    scaled = (w * np.exp2(127.0 - byte)[:, None, :]).reshape(k, n).astype(np.float32)
    words = np.ascontiguousarray(scaled.reshape(k // 512, 128, 4, n).transpose(0, 1, 3, 2)).astype(ml_dtypes.float8_e4m3fn).view(np.uint8)
    return words, np.ascontiguousarray(byte.astype(np.uint8).reshape(k // 512, 16, n))


def unpack_weight(words, scales):
    g, p, n, _ = words.shape
    vals = np.ascontiguousarray(words).view(ml_dtypes.float8_e4m3fn).astype(np.float64) * np.repeat(np.exp2(scales.astype(np.float64) - 127.0), 8, axis=1)[..., None]
    return vals.transpose(0, 1, 3, 2).reshape(g * 512, n)


def gelu(v):
    return 0.5 * v * (1.0 + np.tanh(np.sqrt(2.0 / np.pi) * (v + 0.044715 * v**3)))


K, T, E, C, N = 1536, 1024, 4, 256, 384


def by_expert(wq, xq):
    return np.concatenate([wq[e].T @ xq[:, e * C:(e + 1) * C] for e in range(E)], axis=1)


def setup_inputs():
    n = np.random.standard_normal
    s = mx_kscale(K)[:, None]
    packed = [pack_weight(m) for m in n((E, K, N)) / np.sqrt(K) / s[None]]
    return {
        "xT": (n((K, T)) * s).astype(np.float32),
        "w_words": np.stack([m[0] for m in packed]),
        "w_scales": np.stack([m[1] for m in packed]),
        "b": (0.3 * n((N, E))).astype(np.float32),
        "gate": np.tile(np.random.uniform(0.2, 1.0, E * C), (K, 1)).astype(np.float32),
        "offs": striped(np.random.permutation(T)[:E * C]),
    }


def reference(xT, w_words, w_scales, b, gate, offs):
    idx = unstriped(offs)
    w = np.stack([unpack_weight(w_words[e], w_scales[e]) for e in range(E)])
    xq = mxq(f64(gate) * f64(xT)[:, idx], 0, "e4m3")
    y = by_expert(w, xq)
    y = gelu(y + np.repeat(f64(b), C, axis=1))
    out = np.zeros((N, T))
    out[:, idx] = y
    return out

@@ -1,0 +1,154 @@
+from contextlib import ExitStack
+
+import concourse.mybir as mybir
+
+K, T, E, C, N = 1536, 1024, 4, 256, 384
+FLOPS = 2 * K * N * E * C
+BYTES = 4 * K * T + E * K * N + E * (K // 32) * N + 4 * N * E + 4 * E * C + 2 * 128 * (E * C // 16) + 4 * N * T
+
+F32 = mybir.dt.float32
+BF16 = mybir.dt.bfloat16
+I32 = mybir.dt.int32
+U32 = mybir.dt.uint32
+U16 = mybir.dt.uint16
+U8 = mybir.dt.uint8
+FP8X4 = mybir.dt.float8_e4m3fn_x4
+MULT = mybir.AluOpType.mult
+GELU = mybir.ActivationFunctionType.Gelu_apprx_tanh
+
+P = 128
+PACK = 4
+K_PASS = P * PACK
+PASSES = K // K_PASS
+ROW_BLOCKS = N // P
+HALF = 512
+HALVES = E * C // HALF
+EXPERTS_PER_HALF = HALF // C
+LIST_COLS = HALF // 16
+
+
+def tile_moe_pre_lin_gelu_kernel(tc, xT, w_words, w_scales, b, gate, offs, out):
+    nc = tc.nc
+    with ExitStack() as ctx:
+        sb = ctx.enter_context(tc.tile_pool(name="sb", bufs=1))
+        psum = ctx.enter_context(tc.psum_pool(name="psum", bufs=1))
+
+        offsets = sb.tile([P, E * C // 16], U16, name="offsets")
+        nc.sync.dma_start(offsets[:], offs)
+
+        def half_list(h):
+            return offsets[:, h * LIST_COLS:(h + 1) * LIST_COLS]
+
+        w_plane = sb.tile([P, E * PASSES * N], U8, name="w_plane", align_bytes=64)
+        nc.vector.memset(w_plane[:].bitcast(I32), 0)
+
+        x_rows = xT.rearrange("(a p j) t -> a j p t", p=P, j=PACK)
+        x_planes = {}
+        gates = []
+
+        def load_x(a, j):
+            x_planes[a, j] = sb.tile([P, T], F32, name=f"x_{a}_{j}")
+            nc.sync.dma_start(x_planes[a, j][:], x_rows[a, j])
+
+        def load_gate(h):
+            gates.append(sb.tile([P, HALF], F32, name=f"gate_{h}"))
+            nc.sync.dma_start(gates[h][:], gate[0:P, h * HALF:(h + 1) * HALF])
+
+        load_x(0, 0)
+        for h in range(HALVES):
+            load_gate(h)
+        for a in range(PASSES):
+            for j in range(PACK):
+                if (a, j) != (0, 0):
+                    load_x(a, j)
+
+        w_tiles = []
+
+        def load_w(e):
+            w_tiles.append(sb.tile([P, PASSES, N], U32, name=f"w_{e}", align_bytes=64))
+            nc.sync.dma_start(w_tiles[e][:].bitcast(I32), w_words[e].rearrange("a p n r -> p a (n r)").bitcast(I32))
+
+        scale_rows = w_scales.rearrange("e a (q r) n -> r q (e a) n", r=4).bitcast(I32)
+        plane_words = w_plane[:].bitcast(I32).rearrange("p (g n) -> p g n", g=E * PASSES)
+        for r in range(4):
+            nc.sync.dma_start(plane_words[r:P:32], scale_rows[r])
+        bias = sb.tile([P, ROW_BLOCKS, E], F32, name="bias")
+        nc.sync.dma_start(bias[:], b.rearrange("(m p) e -> p m e", p=P))
+        for e in range(E):
+            load_w(e)
+
+        gathered = {}
+        codes = {}
+        scales = {}
+        rounded = {}
+
+        def gather(a, h, j):
+            if j == 0:
+                gathered[a, h] = sb.tile([P, PACK, HALF], F32, name=f"g_{a}_{h}")
+            nc.vector.tensor_tensor(gathered[a, h][:, j, :], x_planes[a, j][:].indirect(half_list(h)), gates[h][:], MULT)
+
+        def interleave(a, h):
+            rounded[a, h] = sb.tile([P, HALF, PACK], BF16, name=f"r_{a}_{h}", align_bytes=64)
+            nc.scalar.copy(rounded[a, h][:], gathered[a, h][:].rearrange("p j s -> p s j"))
+
+        def quantize(a, h):
+            codes[a, h] = sb.tile([P, HALF], U32, name=f"c_{a}_{h}", align_bytes=64)
+            scales[a, h] = sb.tile([P, HALF], U8, name=f"s_{a}_{h}", align_bytes=64)
+            nc.vector.quantize_mx(out=codes[a, h][:].bitcast(FP8X4), scales=scales[a, h][:],
+                                  in_=rounded[a, h][:].rearrange("p s j -> p (s j)"))
+
+        results = {}
+
+        def expert_product(h, m):
+            acc = psum.tile([P, HALF], F32, name=f"acc_{h}_{m}")
+            results[h, m] = sb.tile([P, HALF], F32, name=f"y_{h}_{m}")
+            for i in range(EXPERTS_PER_HALF):
+                e = h * EXPERTS_PER_HALF + i
+                slots = slice(i * C, (i + 1) * C)
+                for a in range(PASSES):
+                    first = (e * PASSES + a) * N + m * P
+                    nc.tensor.matmul_mx(
+                        out=acc[:, slots],
+                        lhsT=w_tiles[e][:, a, m * P:(m + 1) * P].bitcast(FP8X4),
+                        lhsT_scale=w_plane[:, first:first + P],
+                        rhs=codes[a, h][:, slots].bitcast(FP8X4),
+                        rhs_scale=scales[a, h][:, slots],
+                        start=(a == 0),
+                        stop=(a == PASSES - 1),
+                    )
+            for i in range(EXPERTS_PER_HALF):
+                e = h * EXPERTS_PER_HALF + i
+                slots = slice(i * C, (i + 1) * C)
+                nc.scalar.activation(results[h, m][:, slots], acc[:, slots], GELU, bias=bias[:, m, e:e + 1])
+
+        out_tiles = [sb.tile([P, T], F32, name=f"out_{m}") for m in range(ROW_BLOCKS)]
+
+        def scatter(h, m):
+            nc.vector.tensor_copy(out_tiles[m][:].indirect(half_list(h)), results[h, m][:])
+
+        for j in range(PACK):
+            for h in range(HALVES):
+                gather(0, h, j)
+        for h in range(HALVES):
+            interleave(0, h)
+        order = [(a, h) for h in range(HALVES) for a in range(1, PASSES)]
+        pending = [(0, h) for h in range(HALVES)]
+        for a, h in order:
+            for j in range(PACK):
+                gather(a, h, j)
+            interleave(a, h)
+            for item in pending:
+                quantize(*item)
+            pending = [(a, h)]
+            if (a, h) == (1, 1):
+                for m in range(ROW_BLOCKS):
+                    expert_product(0, m)
+        scatter(0, 0)
+        quantize(PASSES - 1, HALVES - 1)
+        for m in range(ROW_BLOCKS):
+            expert_product(1, m)
+        for m in range(1, ROW_BLOCKS):
+            scatter(0, m)
+        for m in range(ROW_BLOCKS):
+            scatter(1, m)
+            nc.sync.dma_start(out[m * P:(m + 1) * P, :], out_tiles[m][:])

@@ -42,6 +42,10 @@ def tile_moe_pre_lin_gelu_kernel(tc, xT, w_words, w_scales, b, gate, offs, out):
         w_plane = sb.tile([P, E * PASSES * N], U8, name="w_plane", align_bytes=64)
         nc.vector.memset(w_plane[:].bitcast(I32), 0)
 
+        warm = sb.tile([P, 2], F32, name="warm")
+        nc.vector.memset(warm[:, 0:1], 0.0)
+        nc.scalar.activation(warm[:, 1:2], warm[:, 0:1], GELU)
+
         x_rows = xT.rearrange("(a p j) t -> a j p t", p=P, j=PACK)
         x_planes = {}
         gates = []
@@ -54,13 +58,11 @@ def tile_moe_pre_lin_gelu_kernel(tc, xT, w_words, w_scales, b, gate, offs, out):
             gates.append(sb.tile([P, HALF], F32, name=f"gate_{h}"))
             nc.sync.dma_start(gates[h][:], gate[0:P, h * HALF:(h + 1) * HALF])
 
-        load_x(0, 0)
-        for h in range(HALVES):
-            load_gate(h)
+        load_gate(0)
         for a in range(PASSES):
             for j in range(PACK):
-                if (a, j) != (0, 0):
-                    load_x(a, j)
+                load_x(a, j)
+        load_gate(1)
 
         w_tiles = []
 
@@ -72,8 +74,10 @@ def tile_moe_pre_lin_gelu_kernel(tc, xT, w_words, w_scales, b, gate, offs, out):
         plane_words = w_plane[:].bitcast(I32).rearrange("p (g n) -> p g n", g=E * PASSES)
         for r in range(4):
             nc.sync.dma_start(plane_words[r:P:32], scale_rows[r])
-        bias = sb.tile([P, ROW_BLOCKS, E], F32, name="bias")
-        nc.sync.dma_start(bias[:], b.rearrange("(m p) e -> p m e", p=P))
+        biases = []
+        for h in range(HALVES):
+            biases.append(sb.tile([P, ROW_BLOCKS, E], F32, name=f"bias_{h}", tag=f"bias_{h}", align_bytes=64))
+            nc.sync.dma_start(biases[h][:], b.rearrange("(m p) e -> p m e", p=P))
         for e in range(E):
             load_w(e)
 
@@ -84,12 +88,14 @@ def tile_moe_pre_lin_gelu_kernel(tc, xT, w_words, w_scales, b, gate, offs, out):
 
         def gather(a, h, j):
             if j == 0:
-                gathered[a, h] = sb.tile([P, PACK, HALF], F32, name=f"g_{a}_{h}")
+                gathered[a, h] = sb.tile([P, PACK, HALF], F32, name=f"g_{a}_{h}", tag=f"g_{a}_{h}", align_bytes=64)
             nc.vector.tensor_tensor(gathered[a, h][:, j, :], x_planes[a, j][:].indirect(half_list(h)), gates[h][:], MULT)
 
         def interleave(a, h):
-            rounded[a, h] = sb.tile([P, HALF, PACK], BF16, name=f"r_{a}_{h}", align_bytes=64)
-            nc.scalar.copy(rounded[a, h][:], gathered[a, h][:].rearrange("p j s -> p s j"))
+            rounded[a, h] = sb.tile([P, HALF, PACK], BF16, name=f"r_{a}_{h}", align_bytes=64,
+                                    tag={(1, 1): "bias_0", (2, 1): "g_1_1"}.get((a, h), f"r_{a}_{h}"))
+            nc.scalar.copy(rounded[a, h][:].rearrange("p (c i) j -> p c j i", i=4),
+                           gathered[a, h][:].rearrange("p j (c i) -> p c j i", i=4))
 
         def quantize(a, h):
             codes[a, h] = sb.tile([P, HALF], U32, name=f"c_{a}_{h}", align_bytes=64)
@@ -119,28 +125,26 @@ def tile_moe_pre_lin_gelu_kernel(tc, xT, w_words, w_scales, b, gate, offs, out):
             for i in range(EXPERTS_PER_HALF):
                 e = h * EXPERTS_PER_HALF + i
                 slots = slice(i * C, (i + 1) * C)
-                nc.scalar.activation(results[h, m][:, slots], acc[:, slots], GELU, bias=bias[:, m, e:e + 1])
+                nc.scalar.activation(results[h, m][:, slots], acc[:, slots], GELU, bias=biases[h][:, m, e:e + 1])
 
-        out_tiles = [sb.tile([P, T], F32, name=f"out_{m}") for m in range(ROW_BLOCKS)]
+        out_tiles = {}
+        out_tags = ["out_0", "g_2_1", "g_1_1"]
 
         def scatter(h, m):
+            if h == 0:
+                out_tiles[m] = sb.tile([P, T], F32, name=f"out_{m}", tag=out_tags[m], align_bytes=64)
             nc.vector.tensor_copy(out_tiles[m][:].indirect(half_list(h)), results[h, m][:])
 
-        for j in range(PACK):
-            for h in range(HALVES):
-                gather(0, h, j)
-        for h in range(HALVES):
-            interleave(0, h)
-        order = [(a, h) for h in range(HALVES) for a in range(1, PASSES)]
-        pending = [(0, h) for h in range(HALVES)]
+        order = [(a, h) for h in range(HALVES) for a in range(PASSES)]
+        pending = None
         for a, h in order:
             for j in range(PACK):
                 gather(a, h, j)
             interleave(a, h)
-            for item in pending:
-                quantize(*item)
-            pending = [(a, h)]
-            if (a, h) == (1, 1):
+            if pending is not None:
+                quantize(*pending)
+            pending = (a, h)
+            if (a, h) == (0, 1):
                 for m in range(ROW_BLOCKS):
                     expert_product(0, m)
         scatter(0, 0)

@@ -55,8 +55,8 @@ def tile_moe_pre_lin_gelu_kernel(tc, xT, w_words, w_scales, b, gate, offs, out):
             nc.sync.dma_start(x_planes[a, j][:], x_rows[a, j])
 
         def load_gate(h):
-            gates.append(sb.tile([P, HALF], F32, name=f"gate_{h}"))
-            nc.sync.dma_start(gates[h][:], gate[0:P, h * HALF:(h + 1) * HALF])
+            gates.append(sb.tile([P, HALF], F32, name=f"gate_{h}", tag=f"gate_{h}", align_bytes=64))
+            (nc.scalar if h == 0 else nc.sync).dma_start(gates[h][:], gate[0:P, h * HALF:(h + 1) * HALF])
 
         load_gate(0)
         for a in range(PASSES):
@@ -92,16 +92,33 @@ def tile_moe_pre_lin_gelu_kernel(tc, xT, w_words, w_scales, b, gate, offs, out):
             nc.vector.tensor_tensor(gathered[a, h][:, j, :], x_planes[a, j][:].indirect(half_list(h)), gates[h][:], MULT)
 
         def interleave(a, h):
-            rounded[a, h] = sb.tile([P, HALF, PACK], BF16, name=f"r_{a}_{h}", align_bytes=64,
-                                    tag={(1, 1): "bias_0", (2, 1): "g_1_1"}.get((a, h), f"r_{a}_{h}"))
-            nc.scalar.copy(rounded[a, h][:].rearrange("p (c i) j -> p c j i", i=4),
+            if (a, h) == (0, 0):
+                both = sb.tile([P, 2 * HALF, PACK], BF16, name="r_both", align_bytes=64)
+                rounded["both"] = both[:]
+                rounded[0, 0] = both[:, :HALF, :]
+                rounded[1, 0] = both[:, HALF:, :]
+            elif (a, h) != (1, 0):
+                rounded[a, h] = sb.tile([P, HALF, PACK], BF16, name=f"r_{a}_{h}", align_bytes=64,
+                                        tag={(1, 1): "bias_0", (2, 1): "g_1_1"}.get((a, h), f"r_{a}_{h}"))[:]
+            nc.scalar.copy(rounded[a, h].rearrange("p (c i) j -> p c j i", i=4),
                            gathered[a, h][:].rearrange("p j (c i) -> p c j i", i=4))
 
         def quantize(a, h):
-            codes[a, h] = sb.tile([P, HALF], U32, name=f"c_{a}_{h}", align_bytes=64)
-            scales[a, h] = sb.tile([P, HALF], U8, name=f"s_{a}_{h}", align_bytes=64)
-            nc.vector.quantize_mx(out=codes[a, h][:].bitcast(FP8X4), scales=scales[a, h][:],
-                                  in_=rounded[a, h][:].rearrange("p s j -> p (s j)"))
+            if (a, h) == (0, 0):
+                return
+            if (a, h) == (1, 0):
+                words = sb.tile([P, 2 * HALF], U32, name="c_both", tag="gate_0", align_bytes=64)
+                plane = sb.tile([P, 2 * HALF], U8, name="s_both", align_bytes=64)
+                nc.vector.quantize_mx(out=words[:].bitcast(FP8X4), scales=plane[:],
+                                      in_=rounded["both"].rearrange("p s j -> p (s j)"))
+                for i in range(2):
+                    codes[i, 0] = words[:, i * HALF:(i + 1) * HALF]
+                    scales[i, 0] = plane[:, i * HALF:(i + 1) * HALF]
+                return
+            codes[a, h] = sb.tile([P, HALF], U32, name=f"c_{a}_{h}", align_bytes=64)[:]
+            scales[a, h] = sb.tile([P, HALF], U8, name=f"s_{a}_{h}", align_bytes=64)[:]
+            nc.vector.quantize_mx(out=codes[a, h].bitcast(FP8X4), scales=scales[a, h],
+                                  in_=rounded[a, h].rearrange("p s j -> p (s j)"))
 
         results = {}
 

from contextlib import ExitStack

import concourse.mybir as mybir

K, T, E, C, N = 1536, 1024, 4, 256, 384
FLOPS = 2 * K * N * E * C
BYTES = 4 * K * T + E * K * N + E * (K // 32) * N + 4 * N * E + 4 * E * C + 2 * 128 * (E * C // 16) + 4 * N * T

F32 = mybir.dt.float32
BF16 = mybir.dt.bfloat16
I32 = mybir.dt.int32
U32 = mybir.dt.uint32
U16 = mybir.dt.uint16
U8 = mybir.dt.uint8
FP8X4 = mybir.dt.float8_e4m3fn_x4
MULT = mybir.AluOpType.mult
GELU = mybir.ActivationFunctionType.Gelu_apprx_tanh

P = 128
PACK = 4
K_PASS = P * PACK
PASSES = K // K_PASS
ROW_BLOCKS = N // P
HALF = 512
HALVES = E * C // HALF
EXPERTS_PER_HALF = HALF // C
LIST_COLS = HALF // 16


def tile_moe_pre_lin_gelu_kernel(tc, xT, w_words, w_scales, b, gate, offs, out):
    nc = tc.nc
    with ExitStack() as ctx:
        sb = ctx.enter_context(tc.tile_pool(name="sb", bufs=1))
        psum = ctx.enter_context(tc.psum_pool(name="psum", bufs=1))

        offsets = sb.tile([P, E * C // 16], U16, name="offsets")
        nc.sync.dma_start(offsets[:], offs)

        def half_list(h):
            return offsets[:, h * LIST_COLS:(h + 1) * LIST_COLS]

        w_plane = sb.tile([P, E * PASSES * N], U8, name="w_plane", align_bytes=64)
        nc.vector.memset(w_plane[:].bitcast(I32), 0)

        warm = sb.tile([P, 2], F32, name="warm")
        nc.vector.memset(warm[:, 0:1], 0.0)
        nc.scalar.activation(warm[:, 1:2], warm[:, 0:1], GELU)

        x_rows = xT.rearrange("(a p j) t -> a j p t", p=P, j=PACK)
        x_planes = {}
        gates = []

        def load_x(a, j):
            x_planes[a, j] = sb.tile([P, T], F32, name=f"x_{a}_{j}")
            nc.sync.dma_start(x_planes[a, j][:], x_rows[a, j])

        def load_gate(h):
            gates.append(sb.tile([P, HALF], F32, name=f"gate_{h}", tag=f"gate_{h}", align_bytes=64))
            (nc.scalar if h == 0 else nc.sync).dma_start(gates[h][:], gate[0:P, h * HALF:(h + 1) * HALF])

        load_gate(0)
        for a in range(PASSES):
            for j in range(PACK):
                load_x(a, j)
        load_gate(1)

        w_tiles = []

        def load_w(e):
            w_tiles.append(sb.tile([P, PASSES, N], U32, name=f"w_{e}", align_bytes=64))
            nc.sync.dma_start(w_tiles[e][:].bitcast(I32), w_words[e].rearrange("a p n r -> p a (n r)").bitcast(I32))

        scale_rows = w_scales.rearrange("e a (q r) n -> r q (e a) n", r=4).bitcast(I32)
        plane_words = w_plane[:].bitcast(I32).rearrange("p (g n) -> p g n", g=E * PASSES)
        for r in range(4):
            nc.sync.dma_start(plane_words[r:P:32], scale_rows[r])
        biases = []
        for h in range(HALVES):
            biases.append(sb.tile([P, ROW_BLOCKS, E], F32, name=f"bias_{h}", tag=f"bias_{h}", align_bytes=64))
            nc.sync.dma_start(biases[h][:], b.rearrange("(m p) e -> p m e", p=P))
        for e in range(E):
            load_w(e)

        gathered = {}
        codes = {}
        scales = {}
        rounded = {}

        def gather(a, h, j):
            if j == 0:
                gathered[a, h] = sb.tile([P, PACK, HALF], F32, name=f"g_{a}_{h}", tag=f"g_{a}_{h}", align_bytes=64)
            nc.vector.tensor_tensor(gathered[a, h][:, j, :], x_planes[a, j][:].indirect(half_list(h)), gates[h][:], MULT)

        def interleave(a, h):
            if (a, h) == (0, 0):
                both = sb.tile([P, 2 * HALF, PACK], BF16, name="r_both", align_bytes=64)
                rounded["both"] = both[:]
                rounded[0, 0] = both[:, :HALF, :]
                rounded[1, 0] = both[:, HALF:, :]
            elif (a, h) != (1, 0):
                rounded[a, h] = sb.tile([P, HALF, PACK], BF16, name=f"r_{a}_{h}", align_bytes=64,
                                        tag={(1, 1): "bias_0", (2, 1): "g_1_1"}.get((a, h), f"r_{a}_{h}"))[:]
            nc.scalar.copy(rounded[a, h].rearrange("p (c i) j -> p c j i", i=4),
                           gathered[a, h][:].rearrange("p j (c i) -> p c j i", i=4))

        def quantize(a, h):
            if (a, h) == (0, 0):
                return
            if (a, h) == (1, 0):
                words = sb.tile([P, 2 * HALF], U32, name="c_both", tag="gate_0", align_bytes=64)
                plane = sb.tile([P, 2 * HALF], U8, name="s_both", align_bytes=64)
                nc.vector.quantize_mx(out=words[:].bitcast(FP8X4), scales=plane[:],
                                      in_=rounded["both"].rearrange("p s j -> p (s j)"))
                for i in range(2):
                    codes[i, 0] = words[:, i * HALF:(i + 1) * HALF]
                    scales[i, 0] = plane[:, i * HALF:(i + 1) * HALF]
                return
            codes[a, h] = sb.tile([P, HALF], U32, name=f"c_{a}_{h}", align_bytes=64)[:]
            scales[a, h] = sb.tile([P, HALF], U8, name=f"s_{a}_{h}", align_bytes=64)[:]
            nc.vector.quantize_mx(out=codes[a, h].bitcast(FP8X4), scales=scales[a, h],
                                  in_=rounded[a, h].rearrange("p s j -> p (s j)"))

        results = {}

        def expert_product(h, m):
            acc = psum.tile([P, HALF], F32, name=f"acc_{h}_{m}")
            results[h, m] = sb.tile([P, HALF], F32, name=f"y_{h}_{m}")
            for i in range(EXPERTS_PER_HALF):
                e = h * EXPERTS_PER_HALF + i
                slots = slice(i * C, (i + 1) * C)
                for a in range(PASSES):
                    first = (e * PASSES + a) * N + m * P
                    nc.tensor.matmul_mx(
                        out=acc[:, slots],
                        lhsT=w_tiles[e][:, a, m * P:(m + 1) * P].bitcast(FP8X4),
                        lhsT_scale=w_plane[:, first:first + P],
                        rhs=codes[a, h][:, slots].bitcast(FP8X4),
                        rhs_scale=scales[a, h][:, slots],
                        start=(a == 0),
                        stop=(a == PASSES - 1),
                    )
            for i in range(EXPERTS_PER_HALF):
                e = h * EXPERTS_PER_HALF + i
                slots = slice(i * C, (i + 1) * C)
                nc.scalar.activation(results[h, m][:, slots], acc[:, slots], GELU, bias=biases[h][:, m, e:e + 1])

        out_tiles = {}
        out_tags = ["out_0", "g_2_1", "g_1_1"]

        def scatter(h, m):
            if h == 0:
                out_tiles[m] = sb.tile([P, T], F32, name=f"out_{m}", tag=out_tags[m], align_bytes=64)
            nc.vector.tensor_copy(out_tiles[m][:].indirect(half_list(h)), results[h, m][:])

        order = [(a, h) for h in range(HALVES) for a in range(PASSES)]
        pending = None
        for a, h in order:
            for j in range(PACK):
                gather(a, h, j)
            interleave(a, h)
            if pending is not None:
                quantize(*pending)
            pending = (a, h)
            if (a, h) == (0, 1):
                for m in range(ROW_BLOCKS):
                    expert_product(0, m)
        scatter(0, 0)
        quantize(PASSES - 1, HALVES - 1)
        for m in range(ROW_BLOCKS):
            expert_product(1, m)
        for m in range(1, ROW_BLOCKS):
            scatter(0, m)
        for m in range(ROW_BLOCKS):
            scatter(1, m)
            nc.sync.dma_start(out[m * P:(m + 1) * P, :], out_tiles[m][:])
